import numpy as np
import ml_dtypes


def mxq(x, axis, fmt="e4m3"):
    dtype, down = {"e4m3": (ml_dtypes.float8_e4m3fn, 7), "e5m2": (ml_dtypes.float8_e5m2, 14)}[fmt]
    v = np.moveaxis(np.asarray(x, np.float32).astype(ml_dtypes.bfloat16).astype(np.float64), axis, -1)
    blocks = v.reshape(v.shape[:-1] + (-1, 32))
    amax = np.abs(blocks).max(-1, keepdims=True)
    byte = np.maximum(np.where(amax > 0, np.frexp(amax)[1] - 1 + 127, 0) - down, 1)
    scale = np.exp2(byte - 127.0)
    codes = (blocks / scale).astype(np.float32).astype(dtype).astype(np.float64)
    return np.moveaxis((codes * scale).reshape(v.shape), -1, axis)


WIDE = False


def mx_kscale(k):
    if not WIDE:
        return np.ones(k)
    levels = np.array([10, -10, 5, -5, 0])
    if k % 512:
        return np.exp2(np.random.permutation(np.resize(levels, k // 32))).repeat(32)
    a = np.empty((k // 512, 16))
    for p in range(k // 512):
        a[p, :8] = np.random.permutation(np.resize(levels, 8))
        for g in range(8):
            far = levels[np.abs(levels - a[p, g]) >= 10]
            a[p, g + 8] = far[np.random.randint(len(far))]
    return np.exp2(a.ravel()).repeat(32)


def f64(x):
    return np.asarray(x).astype(np.float64)


def striped(idx):
    return np.tile(idx.reshape(-1, 16).T, (8, 1)).astype(np.uint16)


def unstriped(offs):
    return offs[:16].T.reshape(-1).astype(np.int64)


def pack_weight(w):
    k, n = w.shape
    w = f64(np.asarray(w, np.float32).astype(ml_dtypes.bfloat16)).reshape(k // 32, 32, n)
    amax = np.abs(w).max(1)
    byte = np.clip(np.where(amax > 0, np.frexp(amax)[1] - 1 + 127 - 7, 1), 1, 254)
    scaled = (w * np.exp2(127.0 - byte)[:, None, :]).reshape(k, n).astype(np.float32)
    words = np.ascontiguousarray(scaled.reshape(k // 512, 128, 4, n).transpose(0, 1, 3, 2)).astype(ml_dtypes.float8_e4m3fn).view(np.uint8)
    return words, np.ascontiguousarray(byte.astype(np.uint8).reshape(k // 512, 16, n))


def unpack_weight(words, scales):
    g, p, n, _ = words.shape
    vals = np.ascontiguousarray(words).view(ml_dtypes.float8_e4m3fn).astype(np.float64) * np.repeat(np.exp2(scales.astype(np.float64) - 127.0), 8, axis=1)[..., None]
    return vals.transpose(0, 1, 3, 2).reshape(g * 512, n)


def planes(y):
    n, m = y.shape
    v = y.astype(np.float32).astype(ml_dtypes.bfloat16).astype(np.float64).reshape(n // 32, 32, m)
    top = np.abs(v).max(1)
    byte = np.clip(np.where(top > 0, np.frexp(top)[1] - 1 + 127 - 7, 1), 1, 254)
    codes = (v * np.exp2(127.0 - byte)[:, None, :]).reshape(n, m).astype(np.float32).astype(ml_dtypes.float8_e4m3fn).view(np.uint8)
    words = codes.reshape(n // 512, 128, 4, m).transpose(0, 1, 3, 2)
    return np.ascontiguousarray(words), np.ascontiguousarray(byte.astype(np.uint8).reshape(n // 512, 16, m))


K, T, S, N, H, W, G, U = 512, 1024, 512, 512, 512, 1024, 1024, 1024


def setup_inputs():
    n = np.random.standard_normal
    s = mx_kscale(K)[:, None]
    u = mx_kscale(H)
    packed_xT = pack_weight(n((K, T)) * s)
    packed_eT = pack_weight(n((K, W)) * s)
    packed_dT = pack_weight(n((K, G)) * s)
    return {
        "x_words": packed_xT[0],
        "x_scales": packed_xT[1],
        "w1": (n((K, N)) / np.sqrt(K) / s).astype(np.float32),
        "e_words": packed_eT[0],
        "e_scales": packed_eT[1],
        "w2": (n((K, N)) / np.sqrt(K) / s).astype(np.float32),
        "d_words": packed_dT[0],
        "d_scales": packed_dT[1],
        "w3": (n((K, N)) / np.sqrt(K) / s).astype(np.float32),
        "wa": (np.random.uniform(0.0, 1.0, (H, S))).astype(np.float32),
        "wb": (np.random.uniform(0.0, 1.0, (H, S))).astype(np.float32),
        "unit": (np.random.uniform(0.6, 1.4, (H, 1)) * u[:, None]).astype(np.float32),
        "w4": (n((H, N)) / np.sqrt(H) / u[:, None]).astype(np.float32),
        "offs": striped(np.random.permutation(T)[:S]),
        "bsa": striped(np.random.permutation(W)[:S]),
        "bsb": striped(np.random.permutation(G)[:S]),
        "cor": striped(np.random.permutation(S)),
        "vt": striped(np.random.permutation(np.concatenate([np.arange(S), np.random.randint(0, S, U - S)]))),
    }


def reference(x_words, x_scales, w1, e_words, e_scales, w2, d_words, d_scales, w3, wa, wb, unit, w4, offs, bsa, bsb, cor, vt):
    xq = unpack_weight(x_words, x_scales)[:, unstriped(offs)]
    y = mxq(f64(w1), 0, "e4m3").T @ xq
    e_bsa = unpack_weight(e_words, e_scales)[:, unstriped(bsa)]
    ye = mxq(f64(w2), 0, "e4m3").T @ e_bsa
    d_bsb = unpack_weight(d_words, d_scales)[:, unstriped(bsb)]
    yd = mxq(f64(w3), 0, "e4m3").T @ d_bsb
    bld = y + f64(wa) * ye + f64(wb) * yd
    zc = bld[:, unstriped(cor)]
    corr = (f64(wa) * f64(wb)) * zc
    mxc = np.maximum(bld, corr)
    fv = mxc[:, unstriped(vt)]
    hid = f64(unit) * fv
    out_0 = mxq(f64(w4), 0, "e4m3").T @ mxq(hid, 0, "e4m3")
    return (out_0,) + planes(out_0)

@@ -1,0 +1,244 @@
+from contextlib import ExitStack
+
+import concourse.mybir as mybir
+
+K, T, S, U = 512, 1024, 512, 1024
+FLOPS = 2 * 512 * 512 * (3 * S + U)
+
+F32 = mybir.dt.float32
+BF16 = mybir.dt.bfloat16
+I32 = mybir.dt.int32
+U32 = mybir.dt.uint32
+U16 = mybir.dt.uint16
+U8 = mybir.dt.uint8
+FP8X4 = mybir.dt.float8_e4m3fn_x4
+MULT = mybir.AluOpType.mult
+ADD = mybir.AluOpType.add
+MAX = mybir.AluOpType.max
+COPY = mybir.ActivationFunctionType.Copy
+
+P = 128
+PACK = 4
+SPARE = 16
+CHUNKS = [128, 256, 256, 256, 128]
+WORD_STORES = {2: 0, 4: 3}
+EARLY = 0
+ON_VECTOR = [(0, 3)]
+FUSED = [3]
+
+
+def tile_picked_yblshap_max_po_kernel(
+    tc, x_words, x_scales, w1, e_words, e_scales, w2, d_words, d_scales, w3, wa, wb, unit, w4,
+    offs, bsa, bsb, cor, vt, out_0, out_1, out_2,
+):
+    nc = tc.nc
+    with ExitStack() as ctx:
+        keep = ctx.enter_context(tc.tile_pool(name="keep", bufs=1))
+        psum = ctx.enter_context(tc.psum_pool(name="psum", bufs=8))
+
+        def sb(name, shape, dtype):
+            return keep.tile(shape, dtype, name=name, align_bytes=64)
+
+        def load_list(name, src):
+            dst = sb(name, list(src.shape), U16)
+            nc.sync.dma_start(dst[:], src)
+            return dst
+
+        def load_words(name, src):
+            dst = sb(name, [P, T], U32)
+            nc.sync.dma_start(dst[:].bitcast(I32), src[0].rearrange("p n t -> p (n t)").bitcast(I32))
+            return dst
+
+        def clear_scales(name):
+            dst = sb(name, [P, T], U8)
+            nc.vector.memset(dst[:].bitcast(I32), 0)
+            return dst
+
+        def load_scales(dst, src):
+            for q in range(4):
+                nc.sync.dma_start(dst[32 * q:32 * q + 4, :].bitcast(I32), src[0, 4 * q:4 * q + 4, :].bitcast(I32))
+
+        def load_rows(name, src, t0, t1):
+            dst = sb(name, [P, t1 - t0, 512], F32)
+            nc.sync.dma_start(dst[:], src.rearrange("(p t) n -> p t n", t=PACK)[:, t0:t1, :])
+            return dst
+
+        def gather_table(name, words, scales, offsets):
+            picked_words = sb(name + "_w", [P, S], U32)
+            picked_scales = sb(name + "_s", [P, S], U8)
+            nc.vector.tensor_copy(picked_words[:], words[:].indirect(offsets[:]))
+            nc.vector.tensor_copy(picked_scales[:], scales[:].indirect(offsets[:]))
+            return picked_words, picked_scales
+
+        def deal_views(dealt, raw, m0, m1):
+            dst = dealt[:].rearrange("p (t m j) -> p m t j", t=PACK, j=PACK)[:, m0:m1]
+            src = raw[:].rearrange("p j (m t) -> p m t j", t=PACK)[:, m0:m1]
+            return dst, src
+
+        def deal_scalar(dealt, raw, m0, m1):
+            dst, src = deal_views(dealt, raw, m0, m1)
+            nc.scalar.activation(dst, src, COPY)
+
+        def deal_vector(dealt, raw, m0, m1):
+            dst, src = deal_views(dealt, raw, m0, m1)
+            nc.vector.tensor_copy(dst, src)
+
+        def quantise(name, src):
+            width = src.shape[1] // PACK
+            codes = sb(name + "_c", [P, width], U32)
+            scales = sb(name + "_s", [P, width], U8)
+            nc.vector.quantize_mx(out=codes[:].bitcast(FP8X4), scales=scales[:], in_=src[:])
+            return codes, scales
+
+        def product(dst, weights, t, moving):
+            cols = slice(P * t, P * (t + 1))
+            nc.tensor.matmul_mx(out=dst, lhsT=weights[0][:, cols].bitcast(FP8X4), lhsT_scale=weights[1][:, cols],
+                                rhs=moving[0][:].bitcast(FP8X4), rhs_scale=moving[1][:], start=True, stop=True)
+
+        def first_products(weights, moving):
+            banks = []
+            for t in range(PACK):
+                bank = psum.tile([P, 512], F32, name="bank")
+                product(bank[:], weights, t, moving)
+                banks.append(bank)
+            return banks
+
+        def interleave(dst, src):
+            nc.vector.tensor_copy(dst[:].rearrange("p (c i t) -> p c t i", i=4, t=PACK),
+                                  src[:].rearrange("p t (c i) -> p c t i", i=4))
+
+        xs, es, ds = clear_scales("xs"), clear_scales("es"), clear_scales("ds")
+        xw = load_words("xw", x_words)
+        offs_sb = load_list("offs", offs)
+        load_scales(xs, x_scales)
+        w1_raw = load_rows("w1_raw", w1, 0, 4)
+        ew = load_words("ew", e_words)
+        bsa_sb = load_list("bsa", bsa)
+        load_scales(es, e_scales)
+        w2_raw = load_rows("w2_raw", w2, 0, 4)
+        dw = load_words("dw", d_words)
+        bsb_sb = load_list("bsb", bsb)
+        load_scales(ds, d_scales)
+        w3_raw = load_rows("w3_raw", w3, 0, 4)
+        wa_sb = [load_rows("wa_lo", wa, 0, 2)]
+        wb_sb = [load_rows("wb_lo", wb, 0, 2)]
+        cor_sb = load_list("cor", cor)
+        vt_sb = load_list("vt", vt)
+        unit_sb = sb("unit", [P, PACK], F32)
+        nc.sync.dma_start(unit_sb[:], unit.rearrange("(p t) o -> p (t o)", t=PACK))
+        w4_raw = load_rows("w4_raw", w4, 0, 4)
+        wa_sb.append(load_rows("wa_hi", wa, 2, 4))
+        wb_sb.append(load_rows("wb_hi", wb, 2, 4))
+
+        bld = [sb("bld%d" % t, [P, S + SPARE], F32) for t in range(PACK)]
+        for t in range(PACK):
+            nc.gpsimd.memset(bld[t][:, S:], 0.0)
+
+        dealt = [sb("dealt%d" % i, [P, PACK * 512], BF16) for i in range(4)]
+
+        xq = gather_table("xq", xw, xs, offs_sb)
+        deal_scalar(dealt[0], w1_raw, 0, P)
+        eq = gather_table("eq", ew, es, bsa_sb)
+        w1q = quantise("w1q", dealt[0])
+        deal_scalar(dealt[1], w2_raw, 0, P)
+        dq = gather_table("dq", dw, ds, bsb_sb)
+        w2q = quantise("w2q", dealt[1])
+        deal_scalar(dealt[2], w3_raw, 0, 48)
+        deal_vector(dealt[2], w3_raw, 48, P)
+        w3q = quantise("w3q", dealt[2])
+        deal_scalar(dealt[3], w4_raw, 0, P)
+
+        starts = [sum(CHUNKS[:c]) for c in range(len(CHUNKS))]
+        planes = [sb("planes%d" % c, [P, PACK, w], BF16) for c, w in enumerate(CHUNKS)]
+        part = [sb("part%d" % t, [P, S], F32) for t in range(PACK)]
+        acc = [sb("acc%d" % t, [P, S], F32) for t in range(PACK)]
+        wab = [sb("wab%d" % t, [P, S], F32) for t in range(PACK)]
+        term = [sb("term%d" % t, [P, S], F32) for t in range(PACK)]
+        zc = [sb("zc%d" % t, [P, S], F32) for t in range(PACK)]
+        corr = [sb("corr%d" % t, [P, S], F32) for t in range(PACK)]
+        mxc = [sb("mxc%d" % t, [P, S], F32) for t in range(PACK)]
+        scaled = [sb("scaled%d" % t, [P, S], F32) for t in range(PACK)]
+
+        def one_product(weights, t, moving):
+            bank = psum.tile([P, 512], F32, name="bank")
+            product(bank[:], weights, t, moving)
+            return bank
+
+        def fetch(c, t):
+            cols = slice(starts[c] // 16, (starts[c] + CHUNKS[c]) // 16)
+            if (c, t) in ON_VECTOR:
+                nc.vector.tensor_copy(planes[c][:, t, :], scaled[t][:].indirect(vt_sb[:, cols]))
+            else:
+                nc.scalar.activation(planes[c][:, t, :], scaled[t][:].indirect(vt_sb[:, cols]), COPY)
+
+        def blend(t):
+            wa_t, wb_t = wa_sb[t // 2][:, t % 2, :], wb_sb[t // 2][:, t % 2, :]
+            ye, y, yd = one_product(w2q, t, eq), one_product(w1q, t, xq), one_product(w3q, t, dq)
+            nc.vector.tensor_tensor(part[t][:], ye[:], wa_t, MULT)
+            nc.vector.tensor_tensor(term[t][:], yd[:], wb_t, MULT)
+            nc.vector.tensor_tensor(acc[t][:], y[:], part[t][:], ADD)
+            nc.gpsimd.tensor_tensor(wab[t][:], wa_t, wb_t, MULT)
+            nc.vector.tensor_tensor(bld[t][:, :S], acc[t][:], term[t][:], ADD)
+            if t not in FUSED:
+                nc.scalar.activation(zc[t][:], bld[t][:].indirect(cor_sb[:]), COPY)
+
+        def correct(t):
+            if t in FUSED:
+                nc.vector.tensor_tensor(corr[t][:], bld[t][:].indirect(cor_sb[:]), wab[t][:], MULT)
+            else:
+                nc.vector.tensor_tensor(corr[t][:], zc[t][:], wab[t][:], MULT)
+            nc.vector.tensor_tensor(mxc[t][:], bld[t][:, :S], corr[t][:], MAX)
+            nc.vector.tensor_scalar(scaled[t][:], mxc[t][:], unit_sb[:, t:t + 1], None, MULT)
+            for c in range(EARLY if t < PACK - 1 else 0):
+                fetch(c, t)
+
+        blend(0)
+        for t in range(1, PACK):
+            blend(t)
+            correct(t - 1)
+        w4q = quantise("w4q", dealt[3])
+        correct(PACK - 1)
+
+        out_rows = out_0.rearrange("(p t) r -> p t r", t=PACK)
+        out_words = out_1[0].rearrange("p n t -> p (n t)").bitcast(I32)
+        out_scales = sb("out_scales", [P, U], U8)
+        codes = sb("codes", [P, U], U32)
+
+        def decode(c):
+            w = CHUNKS[c]
+            for t in range(PACK):
+                if c >= EARLY or t == PACK - 1:
+                    fetch(c, t)
+            hid = sb("hid%d" % c, [P, PACK * w], BF16)
+            interleave(hid, planes[c])
+            hq = quantise("hq%d" % c, hid)
+            res = sb("res%d" % c, [P, PACK, w], F32)
+            per_bank = 512 // w
+            for t0 in range(0, PACK, per_bank):
+                bank = psum.tile([P, 512], F32, name="bank")
+                for i in range(per_bank):
+                    product(bank[:, i * w:(i + 1) * w], w4q, t0 + i, hq)
+                nc.scalar.copy(res[:, t0:t0 + per_bank, :].rearrange("p t r -> p (t r)"), bank[:])
+            nc.sync.dma_start(out_rows[:, :, starts[c]:starts[c] + w], res[:])
+            return res
+
+        def hand_on(c, res):
+            w = CHUNKS[c]
+            cols = slice(starts[c], starts[c] + w)
+            rounded = sb("rounded%d" % c, [P, PACK * w], BF16)
+            interleave(rounded, res)
+            nc.vector.quantize_mx(out=codes[:, cols].bitcast(FP8X4), scales=out_scales[:, cols], in_=rounded[:])
+            if c in WORD_STORES:
+                first = WORD_STORES[c]
+                done = slice(starts[first], starts[c] + w)
+                nc.sync.dma_start(out_words[:, done], codes[:, done].bitcast(I32))
+
+        results = [decode(0), decode(1)]
+        for c in range(2, len(CHUNKS)):
+            results.append(decode(c))
+            hand_on(c - 2, results[c - 2])
+        hand_on(len(CHUNKS) - 2, results[-2])
+        hand_on(len(CHUNKS) - 1, results[-1])
+        for q in range(4):
+            queue = nc.sync if q % 2 == 0 else nc.scalar
+            queue.dma_start(out_2[0, 4 * q:4 * q + 4, :].bitcast(I32), out_scales[32 * q:32 * q + 4, :].bitcast(I32))

@@ -20,11 +20,11 @@ COPY = mybir.ActivationFunctionType.Copy
 P = 128
 PACK = 4
 SPARE = 16
-CHUNKS = [128, 256, 256, 256, 128]
-WORD_STORES = {2: 0, 4: 3}
+CHUNKS = [256, 256, 256, 256]
+WORD_STORES = {1: 0, 2: 2, 3: 3}
 EARLY = 0
 ON_VECTOR = [(0, 3)]
-FUSED = [3]
+FUSED = []
 
 
 def tile_picked_yblshap_max_po_kernel(
@@ -55,8 +55,9 @@ def tile_picked_yblshap_max_po_kernel(
             return dst
 
         def load_scales(dst, src):
-            for q in range(4):
-                nc.sync.dma_start(dst[32 * q:32 * q + 4, :].bitcast(I32), src[0, 4 * q:4 * q + 4, :].bitcast(I32))
+            rows = src[0].bitcast(I32).rearrange("(q r) n -> r q n", r=4)
+            for r in range(4):
+                nc.sync.dma_start(dst[r:P:32, :].bitcast(I32), rows[r])
 
         def load_rows(name, src, t0, t1):
             dst = sb(name, [P, t1 - t0, 512], F32)
@@ -70,18 +71,12 @@ def tile_picked_yblshap_max_po_kernel(
             nc.vector.tensor_copy(picked_scales[:], scales[:].indirect(offsets[:]))
             return picked_words, picked_scales
 
-        def deal_views(dealt, raw, m0, m1):
-            dst = dealt[:].rearrange("p (t m j) -> p m t j", t=PACK, j=PACK)[:, m0:m1]
-            src = raw[:].rearrange("p j (m t) -> p m t j", t=PACK)[:, m0:m1]
-            return dst, src
-
-        def deal_scalar(dealt, raw, m0, m1):
-            dst, src = deal_views(dealt, raw, m0, m1)
+        def deal(name, raw, half):
+            dealt = sb("%s_dealt%d" % (name, half), [P, 2 * 512], BF16)
+            dst = dealt[:].rearrange("p (t m j) -> p m j t", t=2, j=PACK)
+            src = raw[:].rearrange("p j (m h t) -> p h m j t", h=2, t=2)[:, half]
             nc.scalar.activation(dst, src, COPY)
-
-        def deal_vector(dealt, raw, m0, m1):
-            dst, src = deal_views(dealt, raw, m0, m1)
-            nc.vector.tensor_copy(dst, src)
+            return dealt
 
         def quantise(name, src):
             width = src.shape[1] // PACK
@@ -91,21 +86,14 @@ def tile_picked_yblshap_max_po_kernel(
             return codes, scales
 
         def product(dst, weights, t, moving):
-            cols = slice(P * t, P * (t + 1))
-            nc.tensor.matmul_mx(out=dst, lhsT=weights[0][:, cols].bitcast(FP8X4), lhsT_scale=weights[1][:, cols],
+            cols = slice(P * (t % 2), P * (t % 2 + 1))
+            codes, scales = weights[t // 2]
+            nc.tensor.matmul_mx(out=dst, lhsT=codes[:, cols].bitcast(FP8X4), lhsT_scale=scales[:, cols],
                                 rhs=moving[0][:].bitcast(FP8X4), rhs_scale=moving[1][:], start=True, stop=True)
 
-        def first_products(weights, moving):
-            banks = []
-            for t in range(PACK):
-                bank = psum.tile([P, 512], F32, name="bank")
-                product(bank[:], weights, t, moving)
-                banks.append(bank)
-            return banks
-
-        def interleave(dst, src):
-            nc.vector.tensor_copy(dst[:].rearrange("p (c i t) -> p c t i", i=4, t=PACK),
-                                  src[:].rearrange("p t (c i) -> p c t i", i=4))
+        def interleave(dst, src, run):
+            nc.vector.tensor_copy(dst[:].rearrange("p (c i t) -> p c t i", i=run, t=PACK),
+                                  src[:].rearrange("p t (c i) -> p c t i", i=run))
 
         xs, es, ds = clear_scales("xs"), clear_scales("es"), clear_scales("ds")
         xw = load_words("xw", x_words)
@@ -120,33 +108,30 @@ def tile_picked_yblshap_max_po_kernel(
         bsb_sb = load_list("bsb", bsb)
         load_scales(ds, d_scales)
         w3_raw = load_rows("w3_raw", w3, 0, 4)
-        wa_sb = [load_rows("wa_lo", wa, 0, 2)]
-        wb_sb = [load_rows("wb_lo", wb, 0, 2)]
+        wa_lo = load_rows("wa_lo", wa, 0, 2)
+        wb_lo = load_rows("wb_lo", wb, 0, 2)
         cor_sb = load_list("cor", cor)
         vt_sb = load_list("vt", vt)
         unit_sb = sb("unit", [P, PACK], F32)
         nc.sync.dma_start(unit_sb[:], unit.rearrange("(p t) o -> p (t o)", t=PACK))
         w4_raw = load_rows("w4_raw", w4, 0, 4)
-        wa_sb.append(load_rows("wa_hi", wa, 2, 4))
-        wb_sb.append(load_rows("wb_hi", wb, 2, 4))
+        wa_hi = load_rows("wa_hi", wa, 2, 4)
+        wb_hi = load_rows("wb_hi", wb, 2, 4)
+        wa_sb, wb_sb = [wa_lo, wa_hi], [wb_lo, wb_hi]
 
         bld = [sb("bld%d" % t, [P, S + SPARE], F32) for t in range(PACK)]
         for t in range(PACK):
             nc.gpsimd.memset(bld[t][:, S:], 0.0)
 
-        dealt = [sb("dealt%d" % i, [P, PACK * 512], BF16) for i in range(4)]
+        def prepare(name, raw):
+            return [quantise("%s_q%d" % (name, half), deal(name, raw, half)) for half in range(2)]
 
         xq = gather_table("xq", xw, xs, offs_sb)
-        deal_scalar(dealt[0], w1_raw, 0, P)
+        w1q = prepare("w1", w1_raw)
         eq = gather_table("eq", ew, es, bsa_sb)
-        w1q = quantise("w1q", dealt[0])
-        deal_scalar(dealt[1], w2_raw, 0, P)
+        w2q = prepare("w2", w2_raw)
         dq = gather_table("dq", dw, ds, bsb_sb)
-        w2q = quantise("w2q", dealt[1])
-        deal_scalar(dealt[2], w3_raw, 0, 48)
-        deal_vector(dealt[2], w3_raw, 48, P)
-        w3q = quantise("w3q", dealt[2])
-        deal_scalar(dealt[3], w4_raw, 0, P)
+        w3q = prepare("w3", w3_raw)
 
         starts = [sum(CHUNKS[:c]) for c in range(len(CHUNKS))]
         planes = [sb("planes%d" % c, [P, PACK, w], BF16) for c, w in enumerate(CHUNKS)]
@@ -177,7 +162,7 @@ def tile_picked_yblshap_max_po_kernel(
             nc.vector.tensor_tensor(part[t][:], ye[:], wa_t, MULT)
             nc.vector.tensor_tensor(term[t][:], yd[:], wb_t, MULT)
             nc.vector.tensor_tensor(acc[t][:], y[:], part[t][:], ADD)
-            nc.gpsimd.tensor_tensor(wab[t][:], wa_t, wb_t, MULT)
+            nc.vector.tensor_tensor(wab[t][:], wa_t, wb_t, MULT)
             nc.vector.tensor_tensor(bld[t][:, :S], acc[t][:], term[t][:], ADD)
             if t not in FUSED:
                 nc.scalar.activation(zc[t][:], bld[t][:].indirect(cor_sb[:]), COPY)
@@ -188,7 +173,10 @@ def tile_picked_yblshap_max_po_kernel(
             else:
                 nc.vector.tensor_tensor(corr[t][:], zc[t][:], wab[t][:], MULT)
             nc.vector.tensor_tensor(mxc[t][:], bld[t][:, :S], corr[t][:], MAX)
-            nc.vector.tensor_scalar(scaled[t][:], mxc[t][:], unit_sb[:, t:t + 1], None, MULT)
+            if t in [0, 1]:
+                nc.scalar.activation(scaled[t][:], mxc[t][:], COPY, scale=unit_sb[:, t:t + 1])
+            else:
+                nc.vector.tensor_scalar(scaled[t][:], mxc[t][:], unit_sb[:, t:t + 1], None, MULT)
             for c in range(EARLY if t < PACK - 1 else 0):
                 fetch(c, t)
 
@@ -196,7 +184,7 @@ def tile_picked_yblshap_max_po_kernel(
         for t in range(1, PACK):
             blend(t)
             correct(t - 1)
-        w4q = quantise("w4q", dealt[3])
+        w4q = prepare("w4", w4_raw)
         correct(PACK - 1)
 
         out_rows = out_0.rearrange("(p t) r -> p t r", t=PACK)
@@ -210,7 +198,7 @@ def tile_picked_yblshap_max_po_kernel(
                 if c >= EARLY or t == PACK - 1:
                     fetch(c, t)
             hid = sb("hid%d" % c, [P, PACK * w], BF16)
-            interleave(hid, planes[c])
+            interleave(hid, planes[c], 4)
             hq = quantise("hq%d" % c, hid)
             res = sb("res%d" % c, [P, PACK, w], F32)
             per_bank = 512 // w
@@ -226,7 +214,7 @@ def tile_picked_yblshap_max_po_kernel(
             w = CHUNKS[c]
             cols = slice(starts[c], starts[c] + w)
             rounded = sb("rounded%d" % c, [P, PACK * w], BF16)
-            interleave(rounded, res)
+            interleave(rounded, res, 2)
             nc.vector.quantize_mx(out=codes[:, cols].bitcast(FP8X4), scales=out_scales[:, cols], in_=rounded[:])
             if c in WORD_STORES:
                 first = WORD_STORES[c]

@@ -23,8 +23,9 @@ SPARE = 16
 CHUNKS = [256, 256, 256, 256]
 WORD_STORES = {1: 0, 2: 2, 3: 3}
 EARLY = 0
-ON_VECTOR = [(0, 3)]
+ON_VECTOR = [(0, 3), (1, 3)]
 FUSED = []
+WAB_TAGS = ["wab0", "wab1", "term1", "wab3"]
 
 
 def tile_picked_yblshap_max_po_kernel(
@@ -137,7 +138,7 @@ def tile_picked_yblshap_max_po_kernel(
         planes = [sb("planes%d" % c, [P, PACK, w], BF16) for c, w in enumerate(CHUNKS)]
         part = [sb("part%d" % t, [P, S], F32) for t in range(PACK)]
         acc = [sb("acc%d" % t, [P, S], F32) for t in range(PACK)]
-        wab = [sb("wab%d" % t, [P, S], F32) for t in range(PACK)]
+        wab = {}
         term = [sb("term%d" % t, [P, S], F32) for t in range(PACK)]
         zc = [sb("zc%d" % t, [P, S], F32) for t in range(PACK)]
         corr = [sb("corr%d" % t, [P, S], F32) for t in range(PACK)]
@@ -156,13 +157,22 @@ def tile_picked_yblshap_max_po_kernel(
             else:
                 nc.scalar.activation(planes[c][:, t, :], scaled[t][:].indirect(vt_sb[:, cols]), COPY)
 
+        banks = {}
+
+        def weigh(pair):
+            tiles = (2 * pair, 2 * pair + 1)
+            for t in tiles:
+                banks[t] = [one_product(w, t, q) for w, q in ((w2q, eq), (w1q, xq), (w3q, dq))]
+            for t in tiles:
+                wab[t] = keep.tile([P, S], F32, name="wab%d" % t, tag=WAB_TAGS[t], align_bytes=64)
+                nc.gpsimd.tensor_tensor(wab[t][:], wa_sb[pair][:, t % 2, :], wb_sb[pair][:, t % 2, :], MULT)
+            for t in tiles:
+                nc.vector.tensor_tensor(part[t][:], banks[t][0][:], wa_sb[pair][:, t % 2, :], MULT)
+            for t in tiles:
+                nc.vector.tensor_tensor(acc[t][:], banks[t][1][:], part[t][:], ADD)
+
         def blend(t):
-            wa_t, wb_t = wa_sb[t // 2][:, t % 2, :], wb_sb[t // 2][:, t % 2, :]
-            ye, y, yd = one_product(w2q, t, eq), one_product(w1q, t, xq), one_product(w3q, t, dq)
-            nc.vector.tensor_tensor(part[t][:], ye[:], wa_t, MULT)
-            nc.vector.tensor_tensor(term[t][:], yd[:], wb_t, MULT)
-            nc.vector.tensor_tensor(acc[t][:], y[:], part[t][:], ADD)
-            nc.vector.tensor_tensor(wab[t][:], wa_t, wb_t, MULT)
+            nc.vector.tensor_tensor(term[t][:], banks[t][2][:], wb_sb[t // 2][:, t % 2, :], MULT)
             nc.vector.tensor_tensor(bld[t][:, :S], acc[t][:], term[t][:], ADD)
             if t not in FUSED:
                 nc.scalar.activation(zc[t][:], bld[t][:].indirect(cor_sb[:]), COPY)
@@ -173,19 +183,24 @@ def tile_picked_yblshap_max_po_kernel(
             else:
                 nc.vector.tensor_tensor(corr[t][:], zc[t][:], wab[t][:], MULT)
             nc.vector.tensor_tensor(mxc[t][:], bld[t][:, :S], corr[t][:], MAX)
-            if t in [0, 1]:
+            if t in []:
                 nc.scalar.activation(scaled[t][:], mxc[t][:], COPY, scale=unit_sb[:, t:t + 1])
             else:
                 nc.vector.tensor_scalar(scaled[t][:], mxc[t][:], unit_sb[:, t:t + 1], None, MULT)
             for c in range(EARLY if t < PACK - 1 else 0):
                 fetch(c, t)
 
+        weigh(0)
         blend(0)
-        for t in range(1, PACK):
-            blend(t)
-            correct(t - 1)
+        blend(1)
+        weigh(1)
+        blend(2)
+        correct(0)
+        blend(3)
+        correct(1)
         w4q = prepare("w4", w4_raw)
-        correct(PACK - 1)
+        correct(2)
+        correct(3)
 
         out_rows = out_0.rearrange("(p t) r -> p t r", t=PACK)
         out_words = out_1[0].rearrange("p n t -> p (n t)").bitcast(I32)
@@ -207,7 +222,7 @@ def tile_picked_yblshap_max_po_kernel(
                 for i in range(per_bank):
                     product(bank[:, i * w:(i + 1) * w], w4q, t0 + i, hq)
                 nc.scalar.copy(res[:, t0:t0 + per_bank, :].rearrange("p t r -> p (t r)"), bank[:])
-            nc.sync.dma_start(out_rows[:, :, starts[c]:starts[c] + w], res[:])
+                nc.sync.dma_start(out_rows[:, t0:t0 + per_bank, starts[c]:starts[c] + w], res[:, t0:t0 + per_bank, :])
             return res
 
         def hand_on(c, res):

@@ -2,8 +2,11 @@ from contextlib import ExitStack
 
 import concourse.mybir as mybir
 
-K, T, S, U = 512, 1024, 512, 1024
-FLOPS = 2 * 512 * 512 * (3 * S + U)
+ROWS = 512
+TABLE = 1024
+PICKED = 512
+CORNERS = 1024
+FLOPS = 2 * ROWS * ROWS * (3 * PICKED + CORNERS)
 
 F32 = mybir.dt.float32
 BF16 = mybir.dt.bfloat16
@@ -19,13 +22,13 @@ COPY = mybir.ActivationFunctionType.Copy
 
 P = 128
 PACK = 4
+QUADRANT = 32
+PER_COLUMN = 16
+BANK = 512
 SPARE = 16
-CHUNKS = [256, 256, 256, 256]
-WORD_STORES = {1: 0, 2: 2, 3: 3}
-EARLY = 0
-ON_VECTOR = [(0, 3), (1, 3)]
-FUSED = []
-WAB_TAGS = ["wab0", "wab1", "term1", "wab3"]
+CHUNK = 256
+CHUNKS = CORNERS // CHUNK
+VECTOR_FETCHES = 2
 
 
 def tile_picked_yblshap_max_po_kernel(
@@ -37,158 +40,131 @@ def tile_picked_yblshap_max_po_kernel(
         keep = ctx.enter_context(tc.tile_pool(name="keep", bufs=1))
         psum = ctx.enter_context(tc.psum_pool(name="psum", bufs=8))
 
-        def sb(name, shape, dtype):
-            return keep.tile(shape, dtype, name=name, align_bytes=64)
+        def sb(name, shape, dtype, tag=""):
+            return keep.tile(shape, dtype, name=name, tag=tag or name, align_bytes=64)
+
+        def row_tiles(name, width):
+            return [sb("%s%d" % (name, t), [P, width], F32) for t in range(PACK)]
 
         def load_list(name, src):
             dst = sb(name, list(src.shape), U16)
             nc.sync.dma_start(dst[:], src)
             return dst
 
-        def load_words(name, src):
-            dst = sb(name, [P, T], U32)
-            nc.sync.dma_start(dst[:].bitcast(I32), src[0].rearrange("p n t -> p (n t)").bitcast(I32))
-            return dst
-
-        def clear_scales(name):
-            dst = sb(name, [P, T], U8)
+        def cleared_scale_tile(name):
+            dst = sb(name, [P, TABLE], U8)
             nc.vector.memset(dst[:].bitcast(I32), 0)
             return dst
 
-        def load_scales(dst, src):
-            rows = src[0].bitcast(I32).rearrange("(q r) n -> r q n", r=4)
-            for r in range(4):
-                nc.sync.dma_start(dst[r:P:32, :].bitcast(I32), rows[r])
+        def load_table(name, words, list_src, scale_tile, scales, first):
+            word_tile = sb(name + "_words", [P, TABLE], U32)
+            nc.sync.dma_start(word_tile[:].bitcast(I32), words[0].rearrange("p n j -> p (n j)").bitcast(I32))
+            list_tile = load_list(name + "_list", list_src)
+            rows = scales[0].bitcast(I32).rearrange("(q r) n -> r q n", r=PACK)
+            for r in range(PACK):
+                nc.sync.dma_start(scale_tile[first + r:P:QUADRANT, :].bitcast(I32), rows[r])
+            return word_tile, scale_tile, list_tile, first
 
         def load_rows(name, src, t0, t1):
-            dst = sb(name, [P, t1 - t0, 512], F32)
+            dst = sb(name, [P, t1 - t0, src.shape[1]], F32)
             nc.sync.dma_start(dst[:], src.rearrange("(p t) n -> p t n", t=PACK)[:, t0:t1, :])
             return dst
 
-        def gather_table(name, words, scales, offsets):
-            picked_words = sb(name + "_w", [P, S], U32)
-            picked_scales = sb(name + "_s", [P, S], U8)
-            nc.vector.tensor_copy(picked_words[:], words[:].indirect(offsets[:]))
-            nc.vector.tensor_copy(picked_scales[:], scales[:].indirect(offsets[:]))
-            return picked_words, picked_scales
-
-        def deal(name, raw, half):
-            dealt = sb("%s_dealt%d" % (name, half), [P, 2 * 512], BF16)
-            dst = dealt[:].rearrange("p (t m j) -> p m j t", t=2, j=PACK)
-            src = raw[:].rearrange("p j (m h t) -> p h m j t", h=2, t=2)[:, half]
-            nc.scalar.activation(dst, src, COPY)
-            return dealt
+        def pick(name, table):
+            word_tile, scale_tile, list_tile, first = table
+            words = sb(name + "_picked_words", [P, PICKED], U32)
+            scales = sb(name + "_picked_scales", [P, PICKED], U8)
+            nc.vector.tensor_copy(words[:], word_tile[:].indirect(list_tile[:]))
+            nc.vector.tensor_copy(scales[:], scale_tile[:].indirect(list_tile[:]))
+            return words[:], scales[first:P, :]
 
         def quantise(name, src):
             width = src.shape[1] // PACK
-            codes = sb(name + "_c", [P, width], U32)
-            scales = sb(name + "_s", [P, width], U8)
-            nc.vector.quantize_mx(out=codes[:].bitcast(FP8X4), scales=scales[:], in_=src[:])
-            return codes, scales
+            words = sb(name + "_words", [P, width], U32)
+            scales = sb(name + "_scales", [P, width], U8)
+            nc.vector.quantize_mx(out=words[:].bitcast(FP8X4), scales=scales[:], in_=src[:])
+            return words[:], scales[:]
 
-        def product(dst, weights, t, moving):
+        def prepare_weight(name, raw):
+            halves = []
+            for h in range(2):
+                dealt = sb("%s_dealt%d" % (name, h), [P, 2 * P * PACK], BF16)
+                nc.scalar.activation(dealt[:].rearrange("p (s m j) -> p m j s", s=2, j=PACK),
+                                     raw[:].rearrange("p j (m h s) -> p h m j s", h=2, s=2)[:, h], COPY)
+                halves.append(quantise("%s_q%d" % (name, h), dealt))
+            return halves
+
+        def product(dst, weight, t, moving):
+            words, scales = weight[t // 2]
             cols = slice(P * (t % 2), P * (t % 2 + 1))
-            codes, scales = weights[t // 2]
-            nc.tensor.matmul_mx(out=dst, lhsT=codes[:, cols].bitcast(FP8X4), lhsT_scale=scales[:, cols],
-                                rhs=moving[0][:].bitcast(FP8X4), rhs_scale=moving[1][:], start=True, stop=True)
+            nc.tensor.matmul_mx(out=dst, lhsT=words[:, cols].bitcast(FP8X4), lhsT_scale=scales[:, cols],
+                                rhs=moving[0].bitcast(FP8X4), rhs_scale=moving[1], start=True, stop=True)
 
         def interleave(dst, src, run):
             nc.vector.tensor_copy(dst[:].rearrange("p (c i t) -> p c t i", i=run, t=PACK),
                                   src[:].rearrange("p t (c i) -> p c t i", i=run))
 
-        xs, es, ds = clear_scales("xs"), clear_scales("es"), clear_scales("ds")
-        xw = load_words("xw", x_words)
-        offs_sb = load_list("offs", offs)
-        load_scales(xs, x_scales)
-        w1_raw = load_rows("w1_raw", w1, 0, 4)
-        ew = load_words("ew", e_words)
-        bsa_sb = load_list("bsa", bsa)
-        load_scales(es, e_scales)
-        w2_raw = load_rows("w2_raw", w2, 0, 4)
-        dw = load_words("dw", d_words)
-        bsb_sb = load_list("bsb", bsb)
-        load_scales(ds, d_scales)
-        w3_raw = load_rows("w3_raw", w3, 0, 4)
-        wa_lo = load_rows("wa_lo", wa, 0, 2)
-        wb_lo = load_rows("wb_lo", wb, 0, 2)
-        cor_sb = load_list("cor", cor)
-        vt_sb = load_list("vt", vt)
-        unit_sb = sb("unit", [P, PACK], F32)
+        scale_tiles = [cleared_scale_tile(name) for name in ("x_scales", "e_scales", "d_scales")]
+        x_table = load_table("x", x_words, offs, scale_tiles[0], x_scales, 0)
+        w1_raw = load_rows("w1_raw", w1, 0, PACK)
+        e_table = load_table("e", e_words, bsa, scale_tiles[1], e_scales, 4)
+        w2_raw = load_rows("w2_raw", w2, 0, PACK)
+        d_table = load_table("d", d_words, bsb, scale_tiles[2], d_scales, 8)
+        w3_raw = load_rows("w3_raw", w3, 0, PACK)
+        wa_pairs = [load_rows("wa_pair0", wa, 0, 2)]
+        wb_pairs = [load_rows("wb_pair0", wb, 0, 2)]
+        cor_list = load_list("cor_list", cor)
+        vt_list = load_list("vt_list", vt)
+        unit_sb = sb("unit_sb", [P, PACK], F32)
         nc.sync.dma_start(unit_sb[:], unit.rearrange("(p t) o -> p (t o)", t=PACK))
-        w4_raw = load_rows("w4_raw", w4, 0, 4)
-        wa_hi = load_rows("wa_hi", wa, 2, 4)
-        wb_hi = load_rows("wb_hi", wb, 2, 4)
-        wa_sb, wb_sb = [wa_lo, wa_hi], [wb_lo, wb_hi]
+        w4_raw = load_rows("w4_raw", w4, 0, PACK)
+        wa_pairs.append(load_rows("wa_pair1", wa, 2, PACK))
+        wb_pairs.append(load_rows("wb_pair1", wb, 2, PACK))
 
-        bld = [sb("bld%d" % t, [P, S + SPARE], F32) for t in range(PACK)]
+        bld = row_tiles("bld", PICKED + SPARE)
         for t in range(PACK):
-            nc.gpsimd.memset(bld[t][:, S:], 0.0)
+            nc.gpsimd.memset(bld[t][:, PICKED:], 0.0)
 
-        def prepare(name, raw):
-            return [quantise("%s_q%d" % (name, half), deal(name, raw, half)) for half in range(2)]
+        x_picked = pick("x", x_table)
+        w1_q = prepare_weight("w1", w1_raw)
+        e_picked = pick("e", e_table)
+        w2_q = prepare_weight("w2", w2_raw)
+        d_picked = pick("d", d_table)
+        w3_q = prepare_weight("w3", w3_raw)
 
-        xq = gather_table("xq", xw, xs, offs_sb)
-        w1q = prepare("w1", w1_raw)
-        eq = gather_table("eq", ew, es, bsa_sb)
-        w2q = prepare("w2", w2_raw)
-        dq = gather_table("dq", dw, ds, bsb_sb)
-        w3q = prepare("w3", w3_raw)
+        fetched = [sb("fetched%d" % c, [P, PACK, CHUNK], BF16) for c in range(CHUNKS)]
+        wa_ye, y_wa_ye, wb_yd = row_tiles("wa_ye", PICKED), row_tiles("y_wa_ye", PICKED), row_tiles("wb_yd", PICKED)
+        zc, corr = row_tiles("zc", PICKED), row_tiles("corr", PICKED)
+        mxc, scaled = row_tiles("mxc", PICKED), row_tiles("scaled", PICKED)
+        banks, wa_wb = {}, {}
+        wa_wb_tags = ["wa_wb0", "wa_wb1", "wb_yd1", "y_wa_ye1"]
 
-        starts = [sum(CHUNKS[:c]) for c in range(len(CHUNKS))]
-        planes = [sb("planes%d" % c, [P, PACK, w], BF16) for c, w in enumerate(CHUNKS)]
-        part = [sb("part%d" % t, [P, S], F32) for t in range(PACK)]
-        acc = [sb("acc%d" % t, [P, S], F32) for t in range(PACK)]
-        wab = {}
-        term = [sb("term%d" % t, [P, S], F32) for t in range(PACK)]
-        zc = [sb("zc%d" % t, [P, S], F32) for t in range(PACK)]
-        corr = [sb("corr%d" % t, [P, S], F32) for t in range(PACK)]
-        mxc = [sb("mxc%d" % t, [P, S], F32) for t in range(PACK)]
-        scaled = [sb("scaled%d" % t, [P, S], F32) for t in range(PACK)]
-
-        def one_product(weights, t, moving):
-            bank = psum.tile([P, 512], F32, name="bank")
-            product(bank[:], weights, t, moving)
+        def product_in_bank(weight, t, moving):
+            bank = psum.tile([P, BANK], F32, name="bank")
+            product(bank[:], weight, t, moving)
             return bank
-
-        def fetch(c, t):
-            cols = slice(starts[c] // 16, (starts[c] + CHUNKS[c]) // 16)
-            if (c, t) in ON_VECTOR:
-                nc.vector.tensor_copy(planes[c][:, t, :], scaled[t][:].indirect(vt_sb[:, cols]))
-            else:
-                nc.scalar.activation(planes[c][:, t, :], scaled[t][:].indirect(vt_sb[:, cols]), COPY)
-
-        banks = {}
 
         def weigh(pair):
             tiles = (2 * pair, 2 * pair + 1)
             for t in tiles:
-                banks[t] = [one_product(w, t, q) for w, q in ((w2q, eq), (w1q, xq), (w3q, dq))]
+                banks[t] = [product_in_bank(w, t, q) for w, q in ((w2_q, e_picked), (w1_q, x_picked), (w3_q, d_picked))]
             for t in tiles:
-                wab[t] = keep.tile([P, S], F32, name="wab%d" % t, tag=WAB_TAGS[t], align_bytes=64)
-                nc.gpsimd.tensor_tensor(wab[t][:], wa_sb[pair][:, t % 2, :], wb_sb[pair][:, t % 2, :], MULT)
+                wa_wb[t] = sb("wa_wb%d" % t, [P, PICKED], F32, tag=wa_wb_tags[t])
+                nc.gpsimd.tensor_tensor(wa_wb[t][:], wa_pairs[pair][:, t % 2, :], wb_pairs[pair][:, t % 2, :], MULT)
             for t in tiles:
-                nc.vector.tensor_tensor(part[t][:], banks[t][0][:], wa_sb[pair][:, t % 2, :], MULT)
+                nc.vector.tensor_tensor(wa_ye[t][:], banks[t][0][:], wa_pairs[pair][:, t % 2, :], MULT)
             for t in tiles:
-                nc.vector.tensor_tensor(acc[t][:], banks[t][1][:], part[t][:], ADD)
+                nc.vector.tensor_tensor(y_wa_ye[t][:], banks[t][1][:], wa_ye[t][:], ADD)
 
         def blend(t):
-            nc.vector.tensor_tensor(term[t][:], banks[t][2][:], wb_sb[t // 2][:, t % 2, :], MULT)
-            nc.vector.tensor_tensor(bld[t][:, :S], acc[t][:], term[t][:], ADD)
-            if t not in FUSED:
-                nc.scalar.activation(zc[t][:], bld[t][:].indirect(cor_sb[:]), COPY)
+            nc.vector.tensor_tensor(wb_yd[t][:], banks[t][2][:], wb_pairs[t // 2][:, t % 2, :], MULT)
+            nc.vector.tensor_tensor(bld[t][:, :PICKED], y_wa_ye[t][:], wb_yd[t][:], ADD)
+            nc.scalar.activation(zc[t][:], bld[t][:].indirect(cor_list[:]), COPY)
 
         def correct(t):
-            if t in FUSED:
-                nc.vector.tensor_tensor(corr[t][:], bld[t][:].indirect(cor_sb[:]), wab[t][:], MULT)
-            else:
-                nc.vector.tensor_tensor(corr[t][:], zc[t][:], wab[t][:], MULT)
-            nc.vector.tensor_tensor(mxc[t][:], bld[t][:, :S], corr[t][:], MAX)
-            if t in []:
-                nc.scalar.activation(scaled[t][:], mxc[t][:], COPY, scale=unit_sb[:, t:t + 1])
-            else:
-                nc.vector.tensor_scalar(scaled[t][:], mxc[t][:], unit_sb[:, t:t + 1], None, MULT)
-            for c in range(EARLY if t < PACK - 1 else 0):
-                fetch(c, t)
+            nc.vector.tensor_tensor(corr[t][:], zc[t][:], wa_wb[t][:], MULT)
+            nc.vector.tensor_tensor(mxc[t][:], bld[t][:, :PICKED], corr[t][:], MAX)
+            nc.vector.tensor_scalar(scaled[t][:], mxc[t][:], unit_sb[:, t:t + 1], None, MULT)
 
         weigh(0)
         blend(0)
@@ -198,50 +174,51 @@ def tile_picked_yblshap_max_po_kernel(
         correct(0)
         blend(3)
         correct(1)
-        w4q = prepare("w4", w4_raw)
+        w4_q = prepare_weight("w4", w4_raw)
         correct(2)
         correct(3)
 
         out_rows = out_0.rearrange("(p t) r -> p t r", t=PACK)
-        out_words = out_1[0].rearrange("p n t -> p (n t)").bitcast(I32)
-        out_scales = sb("out_scales", [P, U], U8)
-        codes = sb("codes", [P, U], U32)
+        out_words = out_1[0].rearrange("p n j -> p (n j)").bitcast(I32)
+        result_scales = sb("result_scales", [P, CORNERS], U8)
+        result_words = sb("result_words", [P, CORNERS], U32)
 
         def decode(c):
-            w = CHUNKS[c]
+            entries = vt_list[:, c * CHUNK // PER_COLUMN:(c + 1) * CHUNK // PER_COLUMN]
             for t in range(PACK):
-                if c >= EARLY or t == PACK - 1:
-                    fetch(c, t)
-            hid = sb("hid%d" % c, [P, PACK * w], BF16)
-            interleave(hid, planes[c], 4)
-            hq = quantise("hq%d" % c, hid)
-            res = sb("res%d" % c, [P, PACK, w], F32)
-            per_bank = 512 // w
-            for t0 in range(0, PACK, per_bank):
-                bank = psum.tile([P, 512], F32, name="bank")
-                for i in range(per_bank):
-                    product(bank[:, i * w:(i + 1) * w], w4q, t0 + i, hq)
-                nc.scalar.copy(res[:, t0:t0 + per_bank, :].rearrange("p t r -> p (t r)"), bank[:])
-                nc.sync.dma_start(out_rows[:, t0:t0 + per_bank, starts[c]:starts[c] + w], res[:, t0:t0 + per_bank, :])
-            return res
+                if t == PACK - 1 and c < VECTOR_FETCHES:
+                    nc.vector.tensor_copy(fetched[c][:, t, :], scaled[t][:].indirect(entries))
+                else:
+                    nc.scalar.activation(fetched[c][:, t, :], scaled[t][:].indirect(entries), COPY)
+            hid = sb("hid%d" % c, [P, PACK * CHUNK], BF16)
+            interleave(hid, fetched[c], 4)
+            hid_q = quantise("hid_q%d" % c, hid)
+            result = sb("result%d" % c, [P, PACK, CHUNK], F32)
+            for t0 in range(0, PACK, 2):
+                bank = psum.tile([P, BANK], F32, name="bank")
+                for s in range(2):
+                    product(bank[:, s * CHUNK:(s + 1) * CHUNK], w4_q, t0 + s, hid_q)
+                nc.scalar.copy(result[:, t0:t0 + 2, :].rearrange("p t r -> p (t r)"), bank[:])
+                nc.sync.dma_start(out_rows[:, t0:t0 + 2, c * CHUNK:(c + 1) * CHUNK], result[:, t0:t0 + 2, :])
+            return result
 
-        def hand_on(c, res):
-            w = CHUNKS[c]
-            cols = slice(starts[c], starts[c] + w)
-            rounded = sb("rounded%d" % c, [P, PACK * w], BF16)
-            interleave(rounded, res, 2)
-            nc.vector.quantize_mx(out=codes[:, cols].bitcast(FP8X4), scales=out_scales[:, cols], in_=rounded[:])
-            if c in WORD_STORES:
-                first = WORD_STORES[c]
-                done = slice(starts[first], starts[c] + w)
-                nc.sync.dma_start(out_words[:, done], codes[:, done].bitcast(I32))
+        def hand_on(c, result):
+            cols = slice(c * CHUNK, (c + 1) * CHUNK)
+            rounded = sb("rounded%d" % c, [P, PACK * CHUNK], BF16)
+            interleave(rounded, result, 2)
+            nc.vector.quantize_mx(out=result_words[:, cols].bitcast(FP8X4), scales=result_scales[:, cols], in_=rounded[:])
+            if c > 0:
+                done = slice(0 if c == 1 else cols.start, cols.stop)
+                nc.sync.dma_start(out_words[:, done], result_words[:, done].bitcast(I32))
 
-        results = [decode(0), decode(1)]
-        for c in range(2, len(CHUNKS)):
-            results.append(decode(c))
-            hand_on(c - 2, results[c - 2])
-        hand_on(len(CHUNKS) - 2, results[-2])
-        hand_on(len(CHUNKS) - 1, results[-1])
-        for q in range(4):
+        results = []
+        for c in range(CHUNKS + 2):
+            if c < CHUNKS:
+                results.append(decode(c))
+            if c >= 2:
+                hand_on(c - 2, results[c - 2])
+
+        for q in range(P // QUADRANT):
             queue = nc.sync if q % 2 == 0 else nc.scalar
-            queue.dma_start(out_2[0, 4 * q:4 * q + 4, :].bitcast(I32), out_scales[32 * q:32 * q + 4, :].bitcast(I32))
+            queue.dma_start(out_2[0, PACK * q:PACK * (q + 1), :].bitcast(I32),
+                            result_scales[QUADRANT * q:QUADRANT * q + PACK, :].bitcast(I32))

from contextlib import ExitStack

import concourse.mybir as mybir

ROWS = 512
TABLE = 1024
PICKED = 512
CORNERS = 1024
FLOPS = 2 * ROWS * ROWS * (3 * PICKED + CORNERS)

F32 = mybir.dt.float32
BF16 = mybir.dt.bfloat16
I32 = mybir.dt.int32
U32 = mybir.dt.uint32
U16 = mybir.dt.uint16
U8 = mybir.dt.uint8
FP8X4 = mybir.dt.float8_e4m3fn_x4
MULT = mybir.AluOpType.mult
ADD = mybir.AluOpType.add
MAX = mybir.AluOpType.max
COPY = mybir.ActivationFunctionType.Copy

P = 128
PACK = 4
QUADRANT = 32
PER_COLUMN = 16
BANK = 512
SPARE = 16
CHUNK = 256
CHUNKS = CORNERS // CHUNK
VECTOR_FETCHES = 2


def tile_picked_yblshap_max_po_kernel(
    tc, x_words, x_scales, w1, e_words, e_scales, w2, d_words, d_scales, w3, wa, wb, unit, w4,
    offs, bsa, bsb, cor, vt, out_0, out_1, out_2,
):
    nc = tc.nc
    with ExitStack() as ctx:
        keep = ctx.enter_context(tc.tile_pool(name="keep", bufs=1))
        psum = ctx.enter_context(tc.psum_pool(name="psum", bufs=8))

        def sb(name, shape, dtype, tag=""):
            return keep.tile(shape, dtype, name=name, tag=tag or name, align_bytes=64)

        def row_tiles(name, width):
            return [sb("%s%d" % (name, t), [P, width], F32) for t in range(PACK)]

        def load_list(name, src):
            dst = sb(name, list(src.shape), U16)
            nc.sync.dma_start(dst[:], src)
            return dst

        def cleared_scale_tile(name):
            dst = sb(name, [P, TABLE], U8)
            nc.vector.memset(dst[:].bitcast(I32), 0)
            return dst

        def load_table(name, words, list_src, scale_tile, scales, first):
            word_tile = sb(name + "_words", [P, TABLE], U32)
            nc.sync.dma_start(word_tile[:].bitcast(I32), words[0].rearrange("p n j -> p (n j)").bitcast(I32))
            list_tile = load_list(name + "_list", list_src)
            rows = scales[0].bitcast(I32).rearrange("(q r) n -> r q n", r=PACK)
            for r in range(PACK):
                nc.sync.dma_start(scale_tile[first + r:P:QUADRANT, :].bitcast(I32), rows[r])
            return word_tile, scale_tile, list_tile, first

        def load_rows(name, src, t0, t1):
            dst = sb(name, [P, t1 - t0, src.shape[1]], F32)
            nc.sync.dma_start(dst[:], src.rearrange("(p t) n -> p t n", t=PACK)[:, t0:t1, :])
            return dst

        def pick(name, table):
            word_tile, scale_tile, list_tile, first = table
            words = sb(name + "_picked_words", [P, PICKED], U32)
            scales = sb(name + "_picked_scales", [P, PICKED], U8)
            nc.vector.tensor_copy(words[:], word_tile[:].indirect(list_tile[:]))
            nc.vector.tensor_copy(scales[:], scale_tile[:].indirect(list_tile[:]))
            return words[:], scales[first:P, :]

        def quantise(name, src):
            width = src.shape[1] // PACK
            words = sb(name + "_words", [P, width], U32)
            scales = sb(name + "_scales", [P, width], U8)
            nc.vector.quantize_mx(out=words[:].bitcast(FP8X4), scales=scales[:], in_=src[:])
            return words[:], scales[:]

        def prepare_weight(name, raw):
            halves = []
            for h in range(2):
                dealt = sb("%s_dealt%d" % (name, h), [P, 2 * P * PACK], BF16)
                nc.scalar.activation(dealt[:].rearrange("p (s m j) -> p m j s", s=2, j=PACK),
                                     raw[:].rearrange("p j (m h s) -> p h m j s", h=2, s=2)[:, h], COPY)
                halves.append(quantise("%s_q%d" % (name, h), dealt))
            return halves

        def product(dst, weight, t, moving):
            words, scales = weight[t // 2]
            cols = slice(P * (t % 2), P * (t % 2 + 1))
            nc.tensor.matmul_mx(out=dst, lhsT=words[:, cols].bitcast(FP8X4), lhsT_scale=scales[:, cols],
                                rhs=moving[0].bitcast(FP8X4), rhs_scale=moving[1], start=True, stop=True)

        def interleave(dst, src, run):
            nc.vector.tensor_copy(dst[:].rearrange("p (c i t) -> p c t i", i=run, t=PACK),
                                  src[:].rearrange("p t (c i) -> p c t i", i=run))

        scale_tiles = [cleared_scale_tile(name) for name in ("x_scales", "e_scales", "d_scales")]
        x_table = load_table("x", x_words, offs, scale_tiles[0], x_scales, 0)
        w1_raw = load_rows("w1_raw", w1, 0, PACK)
        e_table = load_table("e", e_words, bsa, scale_tiles[1], e_scales, 4)
        w2_raw = load_rows("w2_raw", w2, 0, PACK)
        d_table = load_table("d", d_words, bsb, scale_tiles[2], d_scales, 8)
        w3_raw = load_rows("w3_raw", w3, 0, PACK)
        wa_pairs = [load_rows("wa_pair0", wa, 0, 2)]
        wb_pairs = [load_rows("wb_pair0", wb, 0, 2)]
        cor_list = load_list("cor_list", cor)
        vt_list = load_list("vt_list", vt)
        unit_sb = sb("unit_sb", [P, PACK], F32)
        nc.sync.dma_start(unit_sb[:], unit.rearrange("(p t) o -> p (t o)", t=PACK))
        w4_raw = load_rows("w4_raw", w4, 0, PACK)
        wa_pairs.append(load_rows("wa_pair1", wa, 2, PACK))
        wb_pairs.append(load_rows("wb_pair1", wb, 2, PACK))

        bld = row_tiles("bld", PICKED + SPARE)
        for t in range(PACK):
            nc.gpsimd.memset(bld[t][:, PICKED:], 0.0)

        x_picked = pick("x", x_table)
        w1_q = prepare_weight("w1", w1_raw)
        e_picked = pick("e", e_table)
        w2_q = prepare_weight("w2", w2_raw)
        d_picked = pick("d", d_table)
        w3_q = prepare_weight("w3", w3_raw)

        fetched = [sb("fetched%d" % c, [P, PACK, CHUNK], BF16) for c in range(CHUNKS)]
        wa_ye, y_wa_ye, wb_yd = row_tiles("wa_ye", PICKED), row_tiles("y_wa_ye", PICKED), row_tiles("wb_yd", PICKED)
        zc, corr = row_tiles("zc", PICKED), row_tiles("corr", PICKED)
        mxc, scaled = row_tiles("mxc", PICKED), row_tiles("scaled", PICKED)
        banks, wa_wb = {}, {}
        wa_wb_tags = ["wa_wb0", "wa_wb1", "wb_yd1", "y_wa_ye1"]

        def product_in_bank(weight, t, moving):
            bank = psum.tile([P, BANK], F32, name="bank")
            product(bank[:], weight, t, moving)
            return bank

        def weigh(pair):
            tiles = (2 * pair, 2 * pair + 1)
            for t in tiles:
                banks[t] = [product_in_bank(w, t, q) for w, q in ((w2_q, e_picked), (w1_q, x_picked), (w3_q, d_picked))]
            for t in tiles:
                wa_wb[t] = sb("wa_wb%d" % t, [P, PICKED], F32, tag=wa_wb_tags[t])
                nc.gpsimd.tensor_tensor(wa_wb[t][:], wa_pairs[pair][:, t % 2, :], wb_pairs[pair][:, t % 2, :], MULT)
            for t in tiles:
                nc.vector.tensor_tensor(wa_ye[t][:], banks[t][0][:], wa_pairs[pair][:, t % 2, :], MULT)
            for t in tiles:
                nc.vector.tensor_tensor(y_wa_ye[t][:], banks[t][1][:], wa_ye[t][:], ADD)

        def blend(t):
            nc.vector.tensor_tensor(wb_yd[t][:], banks[t][2][:], wb_pairs[t // 2][:, t % 2, :], MULT)
            nc.vector.tensor_tensor(bld[t][:, :PICKED], y_wa_ye[t][:], wb_yd[t][:], ADD)
            nc.scalar.activation(zc[t][:], bld[t][:].indirect(cor_list[:]), COPY)

        def correct(t):
            nc.vector.tensor_tensor(corr[t][:], zc[t][:], wa_wb[t][:], MULT)
            nc.vector.tensor_tensor(mxc[t][:], bld[t][:, :PICKED], corr[t][:], MAX)
            nc.vector.tensor_scalar(scaled[t][:], mxc[t][:], unit_sb[:, t:t + 1], None, MULT)

        weigh(0)
        blend(0)
        blend(1)
        weigh(1)
        blend(2)
        correct(0)
        blend(3)
        correct(1)
        w4_q = prepare_weight("w4", w4_raw)
        correct(2)
        correct(3)

        out_rows = out_0.rearrange("(p t) r -> p t r", t=PACK)
        out_words = out_1[0].rearrange("p n j -> p (n j)").bitcast(I32)
        result_scales = sb("result_scales", [P, CORNERS], U8)
        result_words = sb("result_words", [P, CORNERS], U32)

        def decode(c):
            entries = vt_list[:, c * CHUNK // PER_COLUMN:(c + 1) * CHUNK // PER_COLUMN]
            for t in range(PACK):
                if t == PACK - 1 and c < VECTOR_FETCHES:
                    nc.vector.tensor_copy(fetched[c][:, t, :], scaled[t][:].indirect(entries))
                else:
                    nc.scalar.activation(fetched[c][:, t, :], scaled[t][:].indirect(entries), COPY)
            hid = sb("hid%d" % c, [P, PACK * CHUNK], BF16)
            interleave(hid, fetched[c], 4)
            hid_q = quantise("hid_q%d" % c, hid)
            result = sb("result%d" % c, [P, PACK, CHUNK], F32)
            for t0 in range(0, PACK, 2):
                bank = psum.tile([P, BANK], F32, name="bank")
                for s in range(2):
                    product(bank[:, s * CHUNK:(s + 1) * CHUNK], w4_q, t0 + s, hid_q)
                nc.scalar.copy(result[:, t0:t0 + 2, :].rearrange("p t r -> p (t r)"), bank[:])
                nc.sync.dma_start(out_rows[:, t0:t0 + 2, c * CHUNK:(c + 1) * CHUNK], result[:, t0:t0 + 2, :])
            return result

        def hand_on(c, result):
            cols = slice(c * CHUNK, (c + 1) * CHUNK)
            rounded = sb("rounded%d" % c, [P, PACK * CHUNK], BF16)
            interleave(rounded, result, 2)
            nc.vector.quantize_mx(out=result_words[:, cols].bitcast(FP8X4), scales=result_scales[:, cols], in_=rounded[:])
            if c > 0:
                done = slice(0 if c == 1 else cols.start, cols.stop)
                nc.sync.dma_start(out_words[:, done], result_words[:, done].bitcast(I32))

        results = []
        for c in range(CHUNKS + 2):
            if c < CHUNKS:
                results.append(decode(c))
            if c >= 2:
                hand_on(c - 2, results[c - 2])

        for q in range(P // QUADRANT):
            queue = nc.sync if q % 2 == 0 else nc.scalar
            queue.dma_start(out_2[0, PACK * q:PACK * (q + 1), :].bitcast(I32),
                            result_scales[QUADRANT * q:QUADRANT * q + PACK, :].bitcast(I32))
